import numpy as np
import ml_dtypes


def mxq(x, axis, fmt="e4m3"):
    dtype, down = {"e4m3": (ml_dtypes.float8_e4m3fn, 7), "e5m2": (ml_dtypes.float8_e5m2, 14)}[fmt]
    v = np.moveaxis(np.asarray(x, np.float32).astype(ml_dtypes.bfloat16).astype(np.float64), axis, -1)
    blocks = v.reshape(v.shape[:-1] + (-1, 32))
    amax = np.abs(blocks).max(-1, keepdims=True)
    byte = np.maximum(np.where(amax > 0, np.frexp(amax)[1] - 1 + 127, 0) - down, 1)
    scale = np.exp2(byte - 127.0)
    codes = (blocks / scale).astype(np.float32).astype(dtype).astype(np.float64)
    return np.moveaxis((codes * scale).reshape(v.shape), -1, axis)


WIDE = False


def mx_kscale(k):
    if not WIDE:
        return np.ones(k)
    levels = np.array([10, -10, 5, -5, 0])
    if k % 512:
        return np.exp2(np.random.permutation(np.resize(levels, k // 32))).repeat(32)
    a = np.empty((k // 512, 16))
    for p in range(k // 512):
        a[p, :8] = np.random.permutation(np.resize(levels, 8))
        for g in range(8):
            far = levels[np.abs(levels - a[p, g]) >= 10]
            a[p, g + 8] = far[np.random.randint(len(far))]
    return np.exp2(a.ravel()).repeat(32)


def f64(x):
    return np.asarray(x).astype(np.float64)


def striped(idx):
    return np.tile(idx.reshape(-1, 16).T, (8, 1)).astype(np.uint16)


def unstriped(offs):
    return offs[:16].T.reshape(-1).astype(np.int64)


E2M1 = np.array([0.0, 0.5, 1.0, 1.5, 2.0, 3.0, 4.0, 6.0, -0.0, -0.5, -1.0, -1.5, -2.0, -3.0, -4.0, -6.0])


def pack_weight(w, fmt):
    k, n = w.shape
    w = f64(np.asarray(w, np.float32).astype(ml_dtypes.bfloat16)).reshape(k // 32, 32, n)
    amax = np.abs(w).max(1)
    if fmt == "e4m3":
        byte = np.frexp(amax)[1] - 1 + 127 - 7
    else:
        mant, ex = np.frexp(amax / 6.0)
        byte = np.where(mant > 0.5, ex, ex - 1) + 127
    byte = np.clip(np.where(amax > 0, byte, 1), 1, 254)
    scaled = (w * np.exp2(127.0 - byte)[:, None, :]).reshape(k, n).astype(np.float32)
    by_word = np.ascontiguousarray(scaled.reshape(k // 512, 128, 4, n).transpose(0, 1, 3, 2))
    if fmt == "e4m3":
        words = by_word.astype(ml_dtypes.float8_e4m3fn).view(np.uint8)
    else:
        c = by_word.astype(ml_dtypes.float4_e2m1fn).view(np.uint8) & 0xF
        words = (c[..., 0::2] | (c[..., 1::2] << 4)).reshape(k // 512, 128, 2 * n)
    return np.ascontiguousarray(words), np.ascontiguousarray(byte.astype(np.uint8).reshape(k // 512, 16, n))


def unpack_weight(words, scales, fmt):
    g, _, n = scales.shape
    words = np.ascontiguousarray(words).reshape(g, 128, n, -1)
    if fmt == "e4m3":
        vals = words.view(ml_dtypes.float8_e4m3fn).astype(np.float64)
    else:
        nib = np.empty((g, 128, n, 4), np.uint8)
        nib[..., 0::2] = words & 0xF
        nib[..., 1::2] = words >> 4
        vals = E2M1[nib]
    vals = vals * np.repeat(np.exp2(scales.astype(np.float64) - 127.0), 8, axis=1)[..., None]
    return vals.transpose(0, 1, 3, 2).reshape(g * 512, n)


def gelu(v):
    return 0.5 * v * (1.0 + np.tanh(np.sqrt(2.0 / np.pi) * (v + 0.044715 * v**3)))


def striped8(idx):
    return np.concatenate([v.reshape(-1, 16).T for v in idx]).astype(np.uint16)


def unstriped8(offs):
    return np.stack([offs[16 * g:16 * g + 16].T.reshape(-1) for g in range(8)]).astype(np.int64)


def runs(v, idx8):
    k = np.arange(v.shape[0])
    return v[k[:, None], idx8[k % 512 // 64]]


K, K2, H, N, T, S, T2 = 1024, 512, 1024, 512, 2048, 1024, 2048

def setup_inputs():
    n = np.random.standard_normal
    s1, s2 = mx_kscale(K)[:, None], mx_kscale(K2)[:, None]
    u = mx_kscale(H)[:, None]
    tab_words, tab_scales = pack_weight(n((K, T)) * s1, "e4m3")
    tab2_words, tab2_scales = pack_weight(n((K2, T)) * s2, "e4m3")
    w1_words, w1_scales = pack_weight(n((K, H)) / np.sqrt(K) / s1, "e2m1")
    return {
        "tab_words": tab_words, "tab_scales": tab_scales,
        "offs": striped8(np.stack([np.random.permutation(T)[:S] for _ in range(8)])),
        "tab2_words": tab2_words, "tab2_scales": tab2_scales,
        "offs2": striped(np.random.permutation(T)[:S]),
        "w1_words": w1_words, "w1_scales": w1_scales,
        "b1": (0.5 * n(H)).astype(np.float32),
        "w2": (0.35 * n((K2, H)) / np.sqrt(K2) / s2).astype(np.float32),
        "b2": np.random.uniform(-1.0, 1.0, H).astype(np.float32),
        "gain": (np.random.uniform(0.5, 1.5, H) * u[:, 0]).astype(np.float32),
        "w3": (n((H, N)) / np.sqrt(H) / u).astype(np.float32),
        "page1": n((N, T2)).astype(np.float32),
        "wgo": np.exp(0.3 * n((128, S))).astype(np.float32),
        "offs3": striped(np.random.permutation(T2)[:S]),
    }

def reference(tab_words, tab_scales, offs, tab2_words, tab2_scales, offs2, w1_words, w1_scales,
              b1, w2, b2, gain, w3, page1, wgo, offs3):
    v = runs(unpack_weight(tab_words, tab_scales, "e4m3"), unstriped8(offs))
    v2 = unpack_weight(tab2_words, tab2_scales, "e4m3")[:, unstriped(offs2)]
    w1 = unpack_weight(w1_words, w1_scales, "e2m1")
    zone = np.tanh((w1.T @ v) + f64(b1)[:, None])
    still = np.sin((mxq(f64(w2), 0, "e4m3").T @ v2) + f64(b2)[:, None])
    h = np.maximum(zone, still) * f64(gain)[:, None]
    y = mxq(f64(w3), 0, "e4m3").T @ mxq(h, 0, "e4m3")
    out = f64(page1).copy()
    out[:, unstriped(offs3)] = np.tile(f64(wgo), (N // 128, 1)) * y
    return out

@@ -1,0 +1,259 @@
+from contextlib import ExitStack
+
+import concourse.mybir as mybir
+from concourse.masks import make_identity
+
+K, K2, H, N, T, S, T2 = 1024, 512, 1024, 512, 2048, 1024, 2048
+FLOPS = 2 * S * (K * H + K2 * H + H * N)
+
+F32 = mybir.dt.float32
+BF16 = mybir.dt.bfloat16
+I32 = mybir.dt.int32
+U32 = mybir.dt.uint32
+U16 = mybir.dt.uint16
+U8 = mybir.dt.uint8
+FP8X4 = mybir.dt.float8_e4m3fn_x4
+FP4X4 = mybir.dt.float4_e2m1fn_x4
+ACT = mybir.ActivationFunctionType
+ALU = mybir.AluOpType
+
+P = 128
+PACK = 4
+KP = P * PACK
+W = 512
+HALVES = S // W
+LCOLS = W // 16
+
+
+def tile_list_zone_still_match_kernel(
+    tc, tab_words, tab_scales, offs, tab2_words, tab2_scales, offs2, w1_words, w1_scales,
+    b1, w2, b2, gain, w3, page1, wgo, offs3, out,
+):
+    nc = tc.nc
+    with ExitStack() as ctx:
+        keep = ctx.enter_context(tc.tile_pool(name="keep", bufs=1))
+        ring = ctx.enter_context(tc.tile_pool(name="ring", bufs=2))
+        psum = ctx.enter_context(tc.psum_pool(name="psum", bufs=1))
+
+        def held(name, shape, dtype):
+            return keep.tile(shape, dtype, name=name, align_bytes=64)
+
+        l1 = keep.tile([P, S // 16], U16, name="l1")
+        l2 = keep.tile([P, S // 16], U16, name="l2")
+        l3 = keep.tile([P, S // 16], U16, name="l3")
+        nc.sync.dma_start(l1[:], offs)
+        nc.sync.dma_start(l2[:], offs2)
+        sc1_win = held("sc1_win", [P, T], U8)
+        sc2_win = held("sc2_win", [P, T], U8)
+        vec_rows = held("vec_rows", [P, 2 * P], F32)
+        w1s_raw = held("w1s_raw", [P, 2 * H], U8)
+        sc1_plane = [held("sc1_plane%d" % a, [P, S], U8) for a in range(2)]
+        nc.gpsimd.memset(sc1_win[:].bitcast(I32), 0)
+        nc.vector.memset(sc2_win[:].bitcast(I32), 0)
+        nc.vector.memset(vec_rows[:], 0.0)
+        nc.vector.memset(w1s_raw[:].bitcast(I32), 0)
+        for a in range(2):
+            nc.vector.memset(sc1_plane[a][:].bitcast(I32), 0)
+        ident = held("ident", [P, P], F32)
+        make_identity(nc, ident[:])
+
+        w2_raw = [ring.tile([P, PACK, KP], F32, name="w2_raw%d" % b, tag="w_raw", bufs=4) for b in range(2)]
+        w3_raw = [ring.tile([P, PACK, N], F32, name="w3_raw%d" % b, tag="w_raw", bufs=4) for b in range(2)]
+        tab2_win = held("tab2_win", [P, T], I32)
+        tab_win = [held("tab_win%d" % a, [P, T], I32) for a in range(2)]
+        w1_raw = held("w1_raw", [P, 2, H // 2], I32)
+        w2_rows = w2.rearrange("(p j) r -> p j r", j=PACK)
+        nc.sync.dma_start(w2_raw[0][:], w2_rows[:, :, 0:KP])
+        for a in range(2):
+            nc.sync.dma_start(sc1_win[:].bitcast(I32)[a:P:8, :], tab_scales[a].bitcast(I32))
+        for d in range(4):
+            nc.sync.dma_start(sc2_win[:].bitcast(I32)[32 * d : 32 * d + 4, :],
+                              tab2_scales[0, 4 * d : 4 * d + 4, :].bitcast(I32))
+        nc.sync.dma_start(w2_raw[1][:], w2_rows[:, :, KP : 2 * KP])
+        nc.sync.dma_start(tab2_win[:], tab2_words[0].rearrange("p t i -> p (t i)").bitcast(I32))
+        for v, vec in enumerate((b1, b2, gain)):
+            nc.sync.dma_start(
+                vec_rows[4 * v : 4 * v + 4, :].rearrange("t (g i) -> t g i", i=8),
+                vec.rearrange("(g t i) -> t g i", t=4, i=8))
+        for d in range(4):
+            nc.sync.dma_start(
+                w1s_raw[:].bitcast(I32)[32 * d : 32 * d + 4, :].rearrange("q (a c) -> q a c", a=2),
+                w1_scales.bitcast(I32)[:, 4 * d : 4 * d + 4, :].rearrange("a q c -> q a c"))
+        nc.sync.dma_start(w1_raw[:], w1_words.bitcast(I32).rearrange("a p c -> p a c"))
+        nc.sync.dma_start(tab_win[0][:], tab_words[0].rearrange("p t i -> p (t i)").bitcast(I32))
+
+        sc1_got = held("sc1_got", [P, S], U8)
+        nc.vector.tensor_copy(sc1_got[:], sc1_win[:].indirect(l1[:]))
+        sc2_got = held("sc2_got", [P, S], U8)
+        nc.vector.tensor_copy(sc2_got[:], sc2_win[:].indirect(l2[:]))
+
+        def move_scale_row(a, m):
+            nc.sync.dma_start(sc1_plane[a][:].bitcast(I32)[m:P:32, :],
+                              sc1_got[:].bitcast(I32)[8 * m + a : P : 32, :])
+
+        for x in range(6):
+            move_scale_row(x // 4, x % 4)
+        nc.sync.dma_start(tab_win[1][:], tab_words[1].rearrange("p t i -> p (t i)").bitcast(I32))
+        for x in range(6, 8):
+            move_scale_row(x // 4, x % 4)
+        w3_rows = w3.rearrange("(b m t i) n -> b t m i n", b=2, t=PACK, i=8)
+        for b in range(2):
+            for t in range(PACK):
+                nc.sync.dma_start(w3_raw[b][:, t, :], w3_rows[b, t])
+        nc.sync.dma_start(l3[:], offs3)
+        wgo_sb = held("wgo_sb", [P, S], F32)
+        nc.sync.dma_start(wgo_sb[:], wgo)
+        pages = [held("page%d" % n, [P, T2], F32) for n in range(N // P)]
+        for n in range(N // P):
+            nc.sync.dma_start(pages[n][:], page1[n * P : (n + 1) * P, :])
+
+        def bank(name):
+            return psum.tile([P, W], F32, name=name, tag="h_bank", bufs=6)
+
+        vec_ps = bank("vec_ps")
+        for b in range(2):
+            nc.tensor.transpose(vec_ps[:, b * P : (b + 1) * P], vec_rows[:, b * P : (b + 1) * P], ident[:])
+        vecs = held("vecs", [P, 2, 16], F32)
+        nc.vector.tensor_copy(vecs[:], vec_ps[:, 0 : 2 * P].rearrange("p (b x) -> p b x", b=2)[:, :, 0:16])
+
+        def gather_words(name, window, lst, c):
+            got = held(name, [P, W], U32)
+            nc.vector.tensor_copy(got[:], window[:].bitcast(U32).indirect(lst[:, c * LCOLS : (c + 1) * LCOLS]))
+            return got
+
+        def quantise(name, rounded):
+            codes = held(name + "_codes", [P, KP], U32)
+            scales = held(name + "_scales", [P, KP], U8)
+            nc.vector.quantize_mx(out=codes[:].bitcast(FP8X4), scales=scales[:], in_=rounded[:])
+            return codes, scales
+
+        def rounded_tile(name):
+            return ring.tile([P, PACK * W], BF16, name=name, tag="rounded", bufs=3, align_bytes=64)
+
+        def round_w2(b):
+            rounded = rounded_tile("w2_bf%d" % b)
+            dst = rounded[:].rearrange("p (t m u e j) -> p t m u j e", t=PACK, m=16, e=2, j=PACK)
+            src = w2_raw[b][:].rearrange("p j (m t u e) -> p t m u j e", t=PACK, u=4, e=2)
+            for t in range(PACK):
+                nc.scalar.copy(dst[:, t], src[:, t])
+            return quantise("w2_%d" % b, rounded)
+
+        def round_w3(b):
+            rounded = rounded_tile("w3_bf%d" % b)
+            nc.scalar.copy(rounded[:].rearrange("p (u e t) -> p u t e", e=2, t=PACK),
+                           w3_raw[b][:].rearrange("p t (u e) -> p u t e", e=2))
+            return quantise("w3_%d" % b, rounded)
+
+        def still(c, b):
+            dst = ring.tile([P, PACK, W], F32, name="still", tag="still", bufs=2)
+            codes, scales = w2_q[b]
+            for t in range(PACK):
+                ps = bank("still_ps")
+                nc.tensor.matmul_mx(
+                    out=ps[:], lhsT=codes[:, t * P : (t + 1) * P].bitcast(FP8X4),
+                    lhsT_scale=scales[:, t * P : (t + 1) * P],
+                    rhs=v2[c][:].bitcast(FP8X4), rhs_scale=sc2_got[:, c * W : (c + 1) * W],
+                    start=True, stop=True)
+                nc.scalar.activation(dst[:, t, :], ps[:], ACT.Sin, bias=vecs[:, b, 4 + t : 5 + t])
+            return dst
+
+        def zone(c, b):
+            dst = ring.tile([P, PACK, W], F32, name="zone", tag="zone", bufs=3)
+            for t in range(PACK):
+                ps = bank("zone_ps")
+                col = (2 * t + b) * P
+                for a in range(2):
+                    nc.tensor.matmul_mx(
+                        out=ps[:], lhsT=w1_p[a][:, 2 * col : 2 * (col + P)].bitcast(FP4X4),
+                        lhsT_scale=w1s_p[:, a * H + col : a * H + col + P],
+                        rhs=v1[a][c][:].bitcast(FP8X4), rhs_scale=sc1_plane[a][:, c * W : (c + 1) * W],
+                        start=(a == 0), stop=(a == 1))
+                nc.scalar.activation(dst[:, t, :], ps[:], ACT.Tanh, bias=vecs[:, b, t : t + 1])
+            return dst
+
+        def stronger(z, s):
+            nc.vector.tensor_tensor(z, z, s, ALU.max)
+
+        def gain_on_vector(c, b, m):
+            rounded = rounded_tile("h_bf")
+            g = vecs[:, b, 8:12].unsqueeze(1).unsqueeze(3).broadcast_to([P, W // 2, PACK, 2])
+            nc.vector.tensor_tensor(rounded[:].rearrange("p (u e t) -> p u t e", e=2, t=PACK),
+                                    m[:].rearrange("p t (u e) -> p u t e", e=2), g, ALU.mult)
+            return rounded
+
+        def gain_on_scalar(c, b, m):
+            flat = ring.tile([P, PACK, W], BF16, name="h_flat", tag="h_flat", bufs=2)
+            for t in range(PACK):
+                nc.scalar.activation(flat[:, t, :], m[:, t, :], ACT.Copy, scale=vecs[:, b, 8 + t : 9 + t])
+            rounded = rounded_tile("h_bf")
+            nc.scalar.copy(rounded[:].rearrange("p (u e t) -> p u t e", e=2, t=PACK),
+                           flat[:].rearrange("p t (u e) -> p u t e", e=2))
+            return rounded
+
+        def features(c, n, h_q, y=None):
+            ps = psum.tile([P, W], F32, name="y_ps", tag="y_bank", bufs=2)
+            for b in range(2):
+                nc.tensor.matmul_mx(
+                    out=ps[:], lhsT=w3_q[b][0][:, n * P : (n + 1) * P].bitcast(FP8X4),
+                    lhsT_scale=w3_q[b][1][:, n * P : (n + 1) * P],
+                    rhs=h_q[b][0][:].bitcast(FP8X4), rhs_scale=h_q[b][1][:],
+                    start=(b == 0), stop=(b == 1))
+            if y is None:
+                y = ring.tile([P, W], F32, name="y", tag="y", bufs=4)[:]
+            nc.scalar.copy(y, ps[:])
+            return y
+
+        def place(c, n, y):
+            nc.vector.tensor_tensor(pages[n][:].indirect(l3[:, c * LCOLS : (c + 1) * LCOLS]),
+                                    y, wgo_sb[:, c * W : (c + 1) * W], ALU.mult)
+
+        w2_q = [round_w2(b) for b in range(2)]
+        v2 = [gather_words("v2_%d" % c, tab2_win, l2, c) for c in range(HALVES)]
+        s00 = still(0, 0)
+        s01 = still(0, 1)
+
+        w1_p = [held("w1_p%d" % a, [P, 2 * H], U8) for a in range(2)]
+        for a in range(2):
+            nc.vector.tensor_copy(w1_p[a][:].bitcast(I32).rearrange("p (t g w) -> p t g w", t=PACK, w=4),
+                                  w1_raw[:, a, :].rearrange("p (g t w) -> p t g w", t=PACK, w=4))
+        w1s_p = held("w1s_p", [P, 2 * H], U8)
+        nc.vector.tensor_copy(w1s_p[:].bitcast(I32).rearrange("p (a t g w) -> p a t g w", a=2, t=PACK, w=2),
+                              w1s_raw[:].bitcast(I32).rearrange("p (a g t w) -> p a t g w", a=2, t=PACK, w=2))
+
+        v1 = [[None] * HALVES for a in range(2)]
+        for a in range(2):
+            v1[a][0] = gather_words("v1_%d_0" % a, tab_win[a], l1, 0)
+        z00 = zone(0, 0)
+        z01 = zone(0, 1)
+        for a in range(2):
+            v1[a][1] = gather_words("v1_%d_1" % a, tab_win[a], l1, 1)
+
+        for t in range(PACK):
+            stronger(z00[:, t, :], s00[:, t, :])
+        h00 = gain_on_vector(0, 0, z00)
+        stronger(z01[:], s01[:])
+        q00 = quantise("h00", h00)
+        h01 = gain_on_vector(0, 1, z01)
+        w3_q = [round_w3(b) for b in range(2)]
+        q01 = quantise("h01", h01)
+        s10 = still(1, 0)
+        z10 = zone(1, 0)
+        qa = (q00, q01)
+        place(0, 0, features(0, 0, qa))
+        s11 = still(1, 1)
+        z11 = zone(1, 1)
+        stronger(z10[:], s10[:])
+        place(0, 1, features(0, 1, qa, s10[:, 0, :]))
+        stronger(z11[:], s11[:])
+        y02 = features(0, 2, qa, s11[:, 0, :])
+        y03 = features(0, 3, qa, s11[:, 1, :])
+        h10 = gain_on_scalar(1, 0, z10)
+        h11 = gain_on_scalar(1, 1, z11)
+        place(0, 2, y02)
+        q10 = quantise("h10", h10)
+        place(0, 3, y03)
+        q11 = quantise("h11", h11)
+        for n in range(N // P):
+            y = features(1, n, (q10, q11))
+            place(1, n, y)
+            nc.sync.dma_start(out[n * P : (n + 1) * P, :], pages[n][:])

@@ -42,39 +42,44 @@ def tile_list_zone_still_match_kernel(
         l2 = keep.tile([P, S // 16], U16, name="l2")
         l3 = keep.tile([P, S // 16], U16, name="l3")
         nc.sync.dma_start(l1[:], offs)
-        nc.sync.dma_start(l2[:], offs2)
+        warm = held("warm", [P, 2], F32)
+        nc.vector.memset(warm[:, 0:1], 0.0)
+        nc.scalar.activation(warm[:, 1:2], warm[:, 0:1], ACT.Silu)
+
         sc1_win = held("sc1_win", [P, T], U8)
-        sc2_win = held("sc2_win", [P, T], U8)
+        sc2_win = ring.tile([P, T], U8, name="sc2_win", tag="code_space0", bufs=1, align_bytes=64)
         vec_rows = held("vec_rows", [P, 2 * P], F32)
         w1s_raw = held("w1s_raw", [P, 2 * H], U8)
         sc1_plane = [held("sc1_plane%d" % a, [P, S], U8) for a in range(2)]
-        nc.gpsimd.memset(sc1_win[:].bitcast(I32), 0)
-        nc.vector.memset(sc2_win[:].bitcast(I32), 0)
-        nc.vector.memset(vec_rows[:], 0.0)
+        nc.gpsimd.memset(vec_rows[:], 0.0)
+        nc.gpsimd.memset(sc2_win[:].bitcast(I32), 0)
         nc.vector.memset(w1s_raw[:].bitcast(I32), 0)
         for a in range(2):
             nc.vector.memset(sc1_plane[a][:].bitcast(I32), 0)
         ident = held("ident", [P, P], F32)
         make_identity(nc, ident[:])
 
-        w2_raw = [ring.tile([P, PACK, KP], F32, name="w2_raw%d" % b, tag="w_raw", bufs=4) for b in range(2)]
-        w3_raw = [ring.tile([P, PACK, N], F32, name="w3_raw%d" % b, tag="w_raw", bufs=4) for b in range(2)]
-        tab2_win = held("tab2_win", [P, T], I32)
+        w2_raw = [ring.tile([P, PACK, KP], F32, name="w2_raw%d" % b, tag="w2_space%d" % b, bufs=1,
+                            align_bytes=64) for b in range(2)]
+        w3_raw = [ring.tile([P, PACK, N], F32, name="w3_raw%d" % b, bufs=1) for b in range(2)]
+        tab2_win = ring.tile([P, T], I32, name="tab2_win", tag="code_space1", bufs=1, align_bytes=64)
         tab_win = [held("tab_win%d" % a, [P, T], I32) for a in range(2)]
         w1_raw = held("w1_raw", [P, 2, H // 2], I32)
         w2_rows = w2.rearrange("(p j) r -> p j r", j=PACK)
-        nc.sync.dma_start(w2_raw[0][:], w2_rows[:, :, 0:KP])
         for a in range(2):
-            nc.sync.dma_start(sc1_win[:].bitcast(I32)[a:P:8, :], tab_scales[a].bitcast(I32))
+            nc.sync.dma_start(sc1_win[:].bitcast(I32)[a:P:2, :],
+                              tab_scales[a].bitcast(I32).unsqueeze(1).broadcast_to([16, 4, T // 4]))
+        nc.sync.dma_start(l2[:], offs2)
+        for v, vec in enumerate((b1, b2, gain)):
+            nc.sync.dma_start(
+                vec_rows[4 * v : 4 * v + 4, :].rearrange("t (g i) -> t g i", i=8),
+                vec.rearrange("(g t i) -> t g i", t=4, i=8))
+        nc.sync.dma_start(w2_raw[0][:], w2_rows[:, :, 0:KP])
         for d in range(4):
             nc.sync.dma_start(sc2_win[:].bitcast(I32)[32 * d : 32 * d + 4, :],
                               tab2_scales[0, 4 * d : 4 * d + 4, :].bitcast(I32))
         nc.sync.dma_start(w2_raw[1][:], w2_rows[:, :, KP : 2 * KP])
         nc.sync.dma_start(tab2_win[:], tab2_words[0].rearrange("p t i -> p (t i)").bitcast(I32))
-        for v, vec in enumerate((b1, b2, gain)):
-            nc.sync.dma_start(
-                vec_rows[4 * v : 4 * v + 4, :].rearrange("t (g i) -> t g i", i=8),
-                vec.rearrange("(g t i) -> t g i", t=4, i=8))
         for d in range(4):
             nc.sync.dma_start(
                 w1s_raw[:].bitcast(I32)[32 * d : 32 * d + 4, :].rearrange("q (a c) -> q a c", a=2),
@@ -114,45 +119,46 @@ def tile_list_zone_still_match_kernel(
         for b in range(2):
             nc.tensor.transpose(vec_ps[:, b * P : (b + 1) * P], vec_rows[:, b * P : (b + 1) * P], ident[:])
         vecs = held("vecs", [P, 2, 16], F32)
-        nc.vector.tensor_copy(vecs[:], vec_ps[:, 0 : 2 * P].rearrange("p (b x) -> p b x", b=2)[:, :, 0:16])
+        nc.scalar.copy(vecs[:], vec_ps[:, 0 : 2 * P].rearrange("p (b x) -> p b x", b=2)[:, :, 0:16])
 
-        def gather_words(name, window, lst, c):
-            got = held(name, [P, W], U32)
-            nc.vector.tensor_copy(got[:], window[:].bitcast(U32).indirect(lst[:, c * LCOLS : (c + 1) * LCOLS]))
+        def gather_words(got, window, lst, c):
+            nc.vector.tensor_copy(got, window[:].bitcast(U32).indirect(lst[:, c * LCOLS : (c + 1) * LCOLS]))
             return got
 
-        def quantise(name, rounded):
-            codes = held(name + "_codes", [P, KP], U32)
+        def quantise(name, rounded, codes=None):
+            if codes is None:
+                codes = held(name + "_codes", [P, KP], U32)
             scales = held(name + "_scales", [P, KP], U8)
             nc.vector.quantize_mx(out=codes[:].bitcast(FP8X4), scales=scales[:], in_=rounded[:])
             return codes, scales
 
         def rounded_tile(name):
-            return ring.tile([P, PACK * W], BF16, name=name, tag="rounded", bufs=3, align_bytes=64)
+            return ring.tile([P, PACK * W], BF16, name=name, tag="rounded", bufs=2, align_bytes=64)
 
         def round_w2(b):
-            rounded = rounded_tile("w2_bf%d" % b)
+            rounded = ring.tile([P, PACK * W], BF16, name="w2_bf%d" % b, tag="w2_bf_space%d" % b, bufs=1,
+                                align_bytes=64)
             dst = rounded[:].rearrange("p (t m u e j) -> p t m u j e", t=PACK, m=16, e=2, j=PACK)
             src = w2_raw[b][:].rearrange("p j (m t u e) -> p t m u j e", t=PACK, u=4, e=2)
             for t in range(PACK):
                 nc.scalar.copy(dst[:, t], src[:, t])
-            return quantise("w2_%d" % b, rounded)
+            return rounded
 
-        def round_w3(b):
-            rounded = rounded_tile("w3_bf%d" % b)
-            nc.scalar.copy(rounded[:].rearrange("p (u e t) -> p u t e", e=2, t=PACK),
+        def round_w3(b, space):
+            rounded = space[:].rearrange("p t w -> p (t w)").bitcast(BF16)[:, b * PACK * W : (b + 1) * PACK * W]
+            nc.scalar.copy(rounded.rearrange("p (u e t) -> p u t e", e=2, t=PACK),
                            w3_raw[b][:].rearrange("p t (u e) -> p u t e", e=2))
             return quantise("w3_%d" % b, rounded)
 
         def still(c, b):
-            dst = ring.tile([P, PACK, W], F32, name="still", tag="still", bufs=2)
+            dst = ring.tile([P, PACK, W], F32, name="still", tag="still", bufs=3, align_bytes=64)
             codes, scales = w2_q[b]
             for t in range(PACK):
                 ps = bank("still_ps")
                 nc.tensor.matmul_mx(
                     out=ps[:], lhsT=codes[:, t * P : (t + 1) * P].bitcast(FP8X4),
                     lhsT_scale=scales[:, t * P : (t + 1) * P],
-                    rhs=v2[c][:].bitcast(FP8X4), rhs_scale=sc2_got[:, c * W : (c + 1) * W],
+                    rhs=v2[c].bitcast(FP8X4), rhs_scale=sc2_got[:, c * W : (c + 1) * W],
                     start=True, stop=True)
                 nc.scalar.activation(dst[:, t, :], ps[:], ACT.Sin, bias=vecs[:, b, 4 + t : 5 + t])
             return dst
@@ -166,7 +172,7 @@ def tile_list_zone_still_match_kernel(
                     nc.tensor.matmul_mx(
                         out=ps[:], lhsT=w1_p[a][:, 2 * col : 2 * (col + P)].bitcast(FP4X4),
                         lhsT_scale=w1s_p[:, a * H + col : a * H + col + P],
-                        rhs=v1[a][c][:].bitcast(FP8X4), rhs_scale=sc1_plane[a][:, c * W : (c + 1) * W],
+                        rhs=v1[a][c].bitcast(FP8X4), rhs_scale=sc1_plane[a][:, c * W : (c + 1) * W],
                         start=(a == 0), stop=(a == 1))
                 nc.scalar.activation(dst[:, t, :], ps[:], ACT.Tanh, bias=vecs[:, b, t : t + 1])
             return dst
@@ -207,26 +213,32 @@ def tile_list_zone_still_match_kernel(
             nc.vector.tensor_tensor(pages[n][:].indirect(l3[:, c * LCOLS : (c + 1) * LCOLS]),
                                     y, wgo_sb[:, c * W : (c + 1) * W], ALU.mult)
 
-        w2_q = [round_w2(b) for b in range(2)]
-        v2 = [gather_words("v2_%d" % c, tab2_win, l2, c) for c in range(HALVES)]
+        def w2_codes(b):
+            return ring.tile([P, KP], U32, name="w2_codes%d" % b, tag="code_space%d" % b, bufs=1, align_bytes=64)
+
+        w2_bf = [round_w2(b) for b in range(2)]
+        w2_q = [quantise("w2_0", w2_bf[0], w2_codes(0))]
+        v2_first = held("v2_first", [P, W], U32)
+        v2_second = ring.tile([P, W], U32, name="v2_second", tag="w2_bf_space0", bufs=1, align_bytes=64)
+        v2 = [gather_words(got[:], tab2_win, l2, c) for c, got in enumerate((v2_first, v2_second))]
+        w2_q.append(quantise("w2_1", w2_bf[1], w2_codes(1)))
         s00 = still(0, 0)
         s01 = still(0, 1)
 
-        w1_p = [held("w1_p%d" % a, [P, 2 * H], U8) for a in range(2)]
+        w1_dealt = ring.tile([P, 3, 2 * H], U8, name="w1_dealt", tag="w2_space0", bufs=1, align_bytes=64)
+        w1_p = [w1_dealt[:, a, :] for a in range(2)]
+        w1s_p = w1_dealt[:, 2, :]
         for a in range(2):
-            nc.vector.tensor_copy(w1_p[a][:].bitcast(I32).rearrange("p (t g w) -> p t g w", t=PACK, w=4),
+            nc.vector.tensor_copy(w1_p[a].bitcast(I32).rearrange("p (t g w) -> p t g w", t=PACK, w=4),
                                   w1_raw[:, a, :].rearrange("p (g t w) -> p t g w", t=PACK, w=4))
-        w1s_p = held("w1s_p", [P, 2 * H], U8)
-        nc.vector.tensor_copy(w1s_p[:].bitcast(I32).rearrange("p (a t g w) -> p a t g w", a=2, t=PACK, w=2),
+        nc.vector.tensor_copy(w1s_p.bitcast(I32).rearrange("p (a t g w) -> p a t g w", a=2, t=PACK, w=2),
                               w1s_raw[:].bitcast(I32).rearrange("p (a g t w) -> p a t g w", a=2, t=PACK, w=2))
 
-        v1 = [[None] * HALVES for a in range(2)]
-        for a in range(2):
-            v1[a][0] = gather_words("v1_%d_0" % a, tab_win[a], l1, 0)
+        v1_all = ring.tile([P, 2 * HALVES, W], U32, name="v1_all", tag="w2_space1", bufs=1, align_bytes=64)
+        v1 = [[gather_words(v1_all[:, HALVES * a + c, :], tab_win[a], l1, c) for c in range(HALVES)]
+              for a in range(2)]
         z00 = zone(0, 0)
         z01 = zone(0, 1)
-        for a in range(2):
-            v1[a][1] = gather_words("v1_%d_1" % a, tab_win[a], l1, 1)
 
         for t in range(PACK):
             stronger(z00[:, t, :], s00[:, t, :])
@@ -234,25 +246,22 @@ def tile_list_zone_still_match_kernel(
         stronger(z01[:], s01[:])
         q00 = quantise("h00", h00)
         h01 = gain_on_vector(0, 1, z01)
-        w3_q = [round_w3(b) for b in range(2)]
         q01 = quantise("h01", h01)
+        w3_q = [round_w3(b, s00) for b in range(2)]
+        qa = (q00, q01)
+        y00 = features(0, 0, qa)
         s10 = still(1, 0)
         z10 = zone(1, 0)
-        qa = (q00, q01)
-        place(0, 0, features(0, 0, qa))
+        stronger(z10[:], s10[:])
+        place(0, 0, y00)
         s11 = still(1, 1)
         z11 = zone(1, 1)
-        stronger(z10[:], s10[:])
-        place(0, 1, features(0, 1, qa, s10[:, 0, :]))
         stronger(z11[:], s11[:])
-        y02 = features(0, 2, qa, s11[:, 0, :])
-        y03 = features(0, 3, qa, s11[:, 1, :])
-        h10 = gain_on_scalar(1, 0, z10)
-        h11 = gain_on_scalar(1, 1, z11)
-        place(0, 2, y02)
-        q10 = quantise("h10", h10)
-        place(0, 3, y03)
-        q11 = quantise("h11", h11)
+        place(0, 1, features(0, 1, qa))
+        q10 = quantise("h10", gain_on_scalar(1, 0, z10))
+        place(0, 2, features(0, 2, qa))
+        q11 = quantise("h11", gain_on_scalar(1, 1, z11))
+        place(0, 3, features(0, 3, qa))
         for n in range(N // P):
             y = features(1, n, (q10, q11))
             place(1, n, y)

from contextlib import ExitStack

import concourse.mybir as mybir
from concourse.masks import make_identity

K, K2, H, N, T, S, T2 = 1024, 512, 1024, 512, 2048, 1024, 2048
FLOPS = 2 * S * (K * H + K2 * H + H * N)

F32 = mybir.dt.float32
BF16 = mybir.dt.bfloat16
I32 = mybir.dt.int32
U32 = mybir.dt.uint32
U16 = mybir.dt.uint16
U8 = mybir.dt.uint8
FP8X4 = mybir.dt.float8_e4m3fn_x4
FP4X4 = mybir.dt.float4_e2m1fn_x4
ACT = mybir.ActivationFunctionType
ALU = mybir.AluOpType

P = 128
PACK = 4
KP = P * PACK
W = 512
HALVES = S // W
LCOLS = W // 16


def tile_list_zone_still_match_kernel(
    tc, tab_words, tab_scales, offs, tab2_words, tab2_scales, offs2, w1_words, w1_scales,
    b1, w2, b2, gain, w3, page1, wgo, offs3, out,
):
    nc = tc.nc
    with ExitStack() as ctx:
        keep = ctx.enter_context(tc.tile_pool(name="keep", bufs=1))
        ring = ctx.enter_context(tc.tile_pool(name="ring", bufs=2))
        psum = ctx.enter_context(tc.psum_pool(name="psum", bufs=1))

        def held(name, shape, dtype):
            return keep.tile(shape, dtype, name=name, align_bytes=64)

        l1 = keep.tile([P, S // 16], U16, name="l1")
        l2 = keep.tile([P, S // 16], U16, name="l2")
        l3 = keep.tile([P, S // 16], U16, name="l3")
        nc.sync.dma_start(l1[:], offs)
        warm = held("warm", [P, 2], F32)
        nc.vector.memset(warm[:, 0:1], 0.0)
        nc.scalar.activation(warm[:, 1:2], warm[:, 0:1], ACT.Silu)

        sc1_win = held("sc1_win", [P, T], U8)
        sc2_win = ring.tile([P, T], U8, name="sc2_win", tag="code_space0", bufs=1, align_bytes=64)
        vec_rows = held("vec_rows", [P, 2 * P], F32)
        w1s_raw = held("w1s_raw", [P, 2 * H], U8)
        sc1_plane = [held("sc1_plane%d" % a, [P, S], U8) for a in range(2)]
        nc.gpsimd.memset(vec_rows[:], 0.0)
        nc.gpsimd.memset(sc2_win[:].bitcast(I32), 0)
        nc.vector.memset(w1s_raw[:].bitcast(I32), 0)
        for a in range(2):
            nc.vector.memset(sc1_plane[a][:].bitcast(I32), 0)
        ident = held("ident", [P, P], F32)
        make_identity(nc, ident[:])

        w2_raw = [ring.tile([P, PACK, KP], F32, name="w2_raw%d" % b, tag="w2_space%d" % b, bufs=1,
                            align_bytes=64) for b in range(2)]
        w3_raw = [ring.tile([P, PACK, N], F32, name="w3_raw%d" % b, bufs=1) for b in range(2)]
        tab2_win = ring.tile([P, T], I32, name="tab2_win", tag="code_space1", bufs=1, align_bytes=64)
        tab_win = [held("tab_win%d" % a, [P, T], I32) for a in range(2)]
        w1_raw = held("w1_raw", [P, 2, H // 2], I32)
        w2_rows = w2.rearrange("(p j) r -> p j r", j=PACK)
        for a in range(2):
            nc.sync.dma_start(sc1_win[:].bitcast(I32)[a:P:2, :],
                              tab_scales[a].bitcast(I32).unsqueeze(1).broadcast_to([16, 4, T // 4]))
        nc.sync.dma_start(l2[:], offs2)
        for v, vec in enumerate((b1, b2, gain)):
            nc.sync.dma_start(
                vec_rows[4 * v : 4 * v + 4, :].rearrange("t (g i) -> t g i", i=8),
                vec.rearrange("(g t i) -> t g i", t=4, i=8))
        nc.sync.dma_start(w2_raw[0][:], w2_rows[:, :, 0:KP])
        for d in range(4):
            nc.sync.dma_start(sc2_win[:].bitcast(I32)[32 * d : 32 * d + 4, :],
                              tab2_scales[0, 4 * d : 4 * d + 4, :].bitcast(I32))
        nc.sync.dma_start(w2_raw[1][:], w2_rows[:, :, KP : 2 * KP])
        nc.sync.dma_start(tab2_win[:], tab2_words[0].rearrange("p t i -> p (t i)").bitcast(I32))
        for d in range(4):
            nc.sync.dma_start(
                w1s_raw[:].bitcast(I32)[32 * d : 32 * d + 4, :].rearrange("q (a c) -> q a c", a=2),
                w1_scales.bitcast(I32)[:, 4 * d : 4 * d + 4, :].rearrange("a q c -> q a c"))
        nc.sync.dma_start(w1_raw[:], w1_words.bitcast(I32).rearrange("a p c -> p a c"))
        nc.sync.dma_start(tab_win[0][:], tab_words[0].rearrange("p t i -> p (t i)").bitcast(I32))

        sc1_got = held("sc1_got", [P, S], U8)
        nc.vector.tensor_copy(sc1_got[:], sc1_win[:].indirect(l1[:]))
        sc2_got = held("sc2_got", [P, S], U8)
        nc.vector.tensor_copy(sc2_got[:], sc2_win[:].indirect(l2[:]))

        def move_scale_row(a, m):
            nc.sync.dma_start(sc1_plane[a][:].bitcast(I32)[m:P:32, :],
                              sc1_got[:].bitcast(I32)[8 * m + a : P : 32, :])

        for x in range(6):
            move_scale_row(x // 4, x % 4)
        nc.sync.dma_start(tab_win[1][:], tab_words[1].rearrange("p t i -> p (t i)").bitcast(I32))
        for x in range(6, 8):
            move_scale_row(x // 4, x % 4)
        w3_rows = w3.rearrange("(b m t i) n -> b t m i n", b=2, t=PACK, i=8)
        for b in range(2):
            for t in range(PACK):
                nc.sync.dma_start(w3_raw[b][:, t, :], w3_rows[b, t])
        nc.sync.dma_start(l3[:], offs3)
        wgo_sb = held("wgo_sb", [P, S], F32)
        nc.sync.dma_start(wgo_sb[:], wgo)
        pages = [held("page%d" % n, [P, T2], F32) for n in range(N // P)]
        for n in range(N // P):
            nc.sync.dma_start(pages[n][:], page1[n * P : (n + 1) * P, :])

        def bank(name):
            return psum.tile([P, W], F32, name=name, tag="h_bank", bufs=6)

        vec_ps = bank("vec_ps")
        for b in range(2):
            nc.tensor.transpose(vec_ps[:, b * P : (b + 1) * P], vec_rows[:, b * P : (b + 1) * P], ident[:])
        vecs = held("vecs", [P, 2, 16], F32)
        nc.scalar.copy(vecs[:], vec_ps[:, 0 : 2 * P].rearrange("p (b x) -> p b x", b=2)[:, :, 0:16])

        def gather_words(got, window, lst, c):
            nc.vector.tensor_copy(got, window[:].bitcast(U32).indirect(lst[:, c * LCOLS : (c + 1) * LCOLS]))
            return got

        def quantise(name, rounded, codes=None):
            if codes is None:
                codes = held(name + "_codes", [P, KP], U32)
            scales = held(name + "_scales", [P, KP], U8)
            nc.vector.quantize_mx(out=codes[:].bitcast(FP8X4), scales=scales[:], in_=rounded[:])
            return codes, scales

        def rounded_tile(name):
            return ring.tile([P, PACK * W], BF16, name=name, tag="rounded", bufs=2, align_bytes=64)

        def round_w2(b):
            rounded = ring.tile([P, PACK * W], BF16, name="w2_bf%d" % b, tag="w2_bf_space%d" % b, bufs=1,
                                align_bytes=64)
            dst = rounded[:].rearrange("p (t m u e j) -> p t m u j e", t=PACK, m=16, e=2, j=PACK)
            src = w2_raw[b][:].rearrange("p j (m t u e) -> p t m u j e", t=PACK, u=4, e=2)
            for t in range(PACK):
                nc.scalar.copy(dst[:, t], src[:, t])
            return rounded

        def round_w3(b, space):
            rounded = space[:].rearrange("p t w -> p (t w)").bitcast(BF16)[:, b * PACK * W : (b + 1) * PACK * W]
            nc.scalar.copy(rounded.rearrange("p (u e t) -> p u t e", e=2, t=PACK),
                           w3_raw[b][:].rearrange("p t (u e) -> p u t e", e=2))
            return quantise("w3_%d" % b, rounded)

        def still(c, b):
            dst = ring.tile([P, PACK, W], F32, name="still", tag="still", bufs=3, align_bytes=64)
            codes, scales = w2_q[b]
            for t in range(PACK):
                ps = bank("still_ps")
                nc.tensor.matmul_mx(
                    out=ps[:], lhsT=codes[:, t * P : (t + 1) * P].bitcast(FP8X4),
                    lhsT_scale=scales[:, t * P : (t + 1) * P],
                    rhs=v2[c].bitcast(FP8X4), rhs_scale=sc2_got[:, c * W : (c + 1) * W],
                    start=True, stop=True)
                nc.scalar.activation(dst[:, t, :], ps[:], ACT.Sin, bias=vecs[:, b, 4 + t : 5 + t])
            return dst

        def zone(c, b):
            dst = ring.tile([P, PACK, W], F32, name="zone", tag="zone", bufs=3)
            for t in range(PACK):
                ps = bank("zone_ps")
                col = (2 * t + b) * P
                for a in range(2):
                    nc.tensor.matmul_mx(
                        out=ps[:], lhsT=w1_p[a][:, 2 * col : 2 * (col + P)].bitcast(FP4X4),
                        lhsT_scale=w1s_p[:, a * H + col : a * H + col + P],
                        rhs=v1[a][c].bitcast(FP8X4), rhs_scale=sc1_plane[a][:, c * W : (c + 1) * W],
                        start=(a == 0), stop=(a == 1))
                nc.scalar.activation(dst[:, t, :], ps[:], ACT.Tanh, bias=vecs[:, b, t : t + 1])
            return dst

        def stronger(z, s):
            nc.vector.tensor_tensor(z, z, s, ALU.max)

        def gain_on_vector(c, b, m):
            rounded = rounded_tile("h_bf")
            g = vecs[:, b, 8:12].unsqueeze(1).unsqueeze(3).broadcast_to([P, W // 2, PACK, 2])
            nc.vector.tensor_tensor(rounded[:].rearrange("p (u e t) -> p u t e", e=2, t=PACK),
                                    m[:].rearrange("p t (u e) -> p u t e", e=2), g, ALU.mult)
            return rounded

        def gain_on_scalar(c, b, m):
            flat = ring.tile([P, PACK, W], BF16, name="h_flat", tag="h_flat", bufs=2)
            for t in range(PACK):
                nc.scalar.activation(flat[:, t, :], m[:, t, :], ACT.Copy, scale=vecs[:, b, 8 + t : 9 + t])
            rounded = rounded_tile("h_bf")
            nc.scalar.copy(rounded[:].rearrange("p (u e t) -> p u t e", e=2, t=PACK),
                           flat[:].rearrange("p t (u e) -> p u t e", e=2))
            return rounded

        def features(c, n, h_q, y=None):
            ps = psum.tile([P, W], F32, name="y_ps", tag="y_bank", bufs=2)
            for b in range(2):
                nc.tensor.matmul_mx(
                    out=ps[:], lhsT=w3_q[b][0][:, n * P : (n + 1) * P].bitcast(FP8X4),
                    lhsT_scale=w3_q[b][1][:, n * P : (n + 1) * P],
                    rhs=h_q[b][0][:].bitcast(FP8X4), rhs_scale=h_q[b][1][:],
                    start=(b == 0), stop=(b == 1))
            if y is None:
                y = ring.tile([P, W], F32, name="y", tag="y", bufs=4)[:]
            nc.scalar.copy(y, ps[:])
            return y

        def place(c, n, y):
            nc.vector.tensor_tensor(pages[n][:].indirect(l3[:, c * LCOLS : (c + 1) * LCOLS]),
                                    y, wgo_sb[:, c * W : (c + 1) * W], ALU.mult)

        def w2_codes(b):
            return ring.tile([P, KP], U32, name="w2_codes%d" % b, tag="code_space%d" % b, bufs=1, align_bytes=64)

        w2_bf = [round_w2(b) for b in range(2)]
        w2_q = [quantise("w2_0", w2_bf[0], w2_codes(0))]
        v2_first = held("v2_first", [P, W], U32)
        v2_second = ring.tile([P, W], U32, name="v2_second", tag="w2_bf_space0", bufs=1, align_bytes=64)
        v2 = [gather_words(got[:], tab2_win, l2, c) for c, got in enumerate((v2_first, v2_second))]
        w2_q.append(quantise("w2_1", w2_bf[1], w2_codes(1)))
        s00 = still(0, 0)
        s01 = still(0, 1)

        w1_dealt = ring.tile([P, 3, 2 * H], U8, name="w1_dealt", tag="w2_space0", bufs=1, align_bytes=64)
        w1_p = [w1_dealt[:, a, :] for a in range(2)]
        w1s_p = w1_dealt[:, 2, :]
        for a in range(2):
            nc.vector.tensor_copy(w1_p[a].bitcast(I32).rearrange("p (t g w) -> p t g w", t=PACK, w=4),
                                  w1_raw[:, a, :].rearrange("p (g t w) -> p t g w", t=PACK, w=4))
        nc.vector.tensor_copy(w1s_p.bitcast(I32).rearrange("p (a t g w) -> p a t g w", a=2, t=PACK, w=2),
                              w1s_raw[:].bitcast(I32).rearrange("p (a g t w) -> p a t g w", a=2, t=PACK, w=2))

        v1_all = ring.tile([P, 2 * HALVES, W], U32, name="v1_all", tag="w2_space1", bufs=1, align_bytes=64)
        v1 = [[gather_words(v1_all[:, HALVES * a + c, :], tab_win[a], l1, c) for c in range(HALVES)]
              for a in range(2)]
        z00 = zone(0, 0)
        z01 = zone(0, 1)

        for t in range(PACK):
            stronger(z00[:, t, :], s00[:, t, :])
        h00 = gain_on_vector(0, 0, z00)
        stronger(z01[:], s01[:])
        q00 = quantise("h00", h00)
        h01 = gain_on_vector(0, 1, z01)
        q01 = quantise("h01", h01)
        w3_q = [round_w3(b, s00) for b in range(2)]
        qa = (q00, q01)
        y00 = features(0, 0, qa)
        s10 = still(1, 0)
        z10 = zone(1, 0)
        stronger(z10[:], s10[:])
        place(0, 0, y00)
        s11 = still(1, 1)
        z11 = zone(1, 1)
        stronger(z11[:], s11[:])
        place(0, 1, features(0, 1, qa))
        q10 = quantise("h10", gain_on_scalar(1, 0, z10))
        place(0, 2, features(0, 2, qa))
        q11 = quantise("h11", gain_on_scalar(1, 1, z11))
        place(0, 3, features(0, 3, qa))
        for n in range(N // P):
            y = features(1, n, (q10, q11))
            place(1, n, y)
            nc.sync.dma_start(out[n * P : (n + 1) * P, :], pages[n][:])
